import numpy as np
import ml_dtypes


def mxq(x, axis, fmt="e4m3"):
    dtype, down = {"e4m3": (ml_dtypes.float8_e4m3fn, 7), "e5m2": (ml_dtypes.float8_e5m2, 14)}[fmt]
    v = np.moveaxis(np.asarray(x, np.float32).astype(ml_dtypes.bfloat16).astype(np.float64), axis, -1)
    blocks = v.reshape(v.shape[:-1] + (-1, 32))
    amax = np.abs(blocks).max(-1, keepdims=True)
    byte = np.maximum(np.where(amax > 0, np.frexp(amax)[1] - 1 + 127, 0) - down, 1)
    scale = np.exp2(byte - 127.0)
    codes = (blocks / scale).astype(np.float32).astype(dtype).astype(np.float64)
    return np.moveaxis((codes * scale).reshape(v.shape), -1, axis)


WIDE = False


def mx_kscale(k):
    if not WIDE:
        return np.ones(k)
    levels = np.array([10, -10, 5, -5, 0])
    if k % 512:
        return np.exp2(np.random.permutation(np.resize(levels, k // 32))).repeat(32)
    a = np.empty((k // 512, 16))
    for p in range(k // 512):
        a[p, :8] = np.random.permutation(np.resize(levels, 8))
        for g in range(8):
            far = levels[np.abs(levels - a[p, g]) >= 10]
            a[p, g + 8] = far[np.random.randint(len(far))]
    return np.exp2(a.ravel()).repeat(32)


def f64(x):
    return np.asarray(x).astype(np.float64)


def striped(idx):
    return np.tile(idx.reshape(-1, 16).T, (8, 1)).astype(np.uint16)


def unstriped(offs):
    return offs[:16].T.reshape(-1).astype(np.int64)


def striped8(idx):
    return np.concatenate([x.reshape(-1, 16).T for x in idx]).astype(np.uint16)


def runs(offs, k):
    lists = np.stack([offs[16 * r : 16 * r + 16].T.reshape(-1) for r in range(8)]).astype(np.int64)
    return lists[np.arange(k) % 512 // 64]


def pack_weight(w):
    k, n = w.shape
    w = f64(np.asarray(w, np.float32).astype(ml_dtypes.bfloat16)).reshape(k // 32, 32, n)
    amax = np.abs(w).max(1)
    byte = np.clip(np.where(amax > 0, np.frexp(amax)[1] - 1 + 127 - 7, 1), 1, 254)
    scaled = (w * np.exp2(127.0 - byte)[:, None, :]).reshape(k, n).astype(np.float32)
    words = np.ascontiguousarray(scaled.reshape(k // 512, 128, 4, n).transpose(0, 1, 3, 2)).astype(ml_dtypes.float8_e4m3fn).view(np.uint8)
    return words, np.ascontiguousarray(byte.astype(np.uint8).reshape(k // 512, 16, n))


def unpack_weight(words, scales):
    g, p, n, _ = words.shape
    vals = np.ascontiguousarray(words).view(ml_dtypes.float8_e4m3fn).astype(np.float64) * np.repeat(np.exp2(scales.astype(np.float64) - 127.0), 8, axis=1)[..., None]
    return vals.transpose(0, 1, 3, 2).reshape(g * 512, n)


K, T, S, N, H, J = 512, 2048, 512, 512, 512, 512


def setup_inputs():
    n = np.random.standard_normal
    s = mx_kscale(K)[:, None]
    u = mx_kscale(S)
    packed_xT = pack_weight(n((K, T)) * s)
    return {
        "x_words": packed_xT[0],
        "x_scales": packed_xT[1],
        "wa": (n((K, H)) / np.sqrt(K) / s).astype(np.float32),
        "tab": n((S, J)).astype(np.float32),
        "gt": (np.random.uniform(0.5, 1.5, (S, 1)) * u[:, None]).astype(np.float32),
        "w1": (n((S, N)) / np.sqrt(S) / u[:, None]).astype(np.float32),
        "offs": striped(np.random.permutation(T)[:S]),
        "n1": striped8(np.random.randint(0, J, (8, H))),
        "n2": striped8(np.random.randint(0, J, (8, H))),
        "n3": striped8(np.stack([np.random.permutation(H) for _ in range(8)])),
        "n4": striped8(np.stack([np.random.permutation(H) for _ in range(8)])),
    }


def reference(x_words, x_scales, wa, tab, gt, w1, offs, n1, n2, n3, n4):
    xq = unpack_weight(x_words, x_scales)[:, unstriped(offs)]
    y = xq.T @ mxq(f64(wa), 0, "e4m3")
    z = f64(gt) * ((y[np.arange(S)[:, None], runs(n3, S)]) * (f64(tab)[np.arange(S)[:, None], runs(n1, S)]) + f64(tab)[np.arange(S)[:, None], runs(n2, S)])
    h = mxq(f64(w1), 0, "e4m3").T @ mxq(z, 0, "e4m3")
    return h - (h[np.arange(N)[:, None], runs(n4, N)])

@@ -1,0 +1,206 @@
+from contextlib import ExitStack
+
+import concourse.mybir as mybir
+
+K, T, S, N, H = 512, 2048, 512, 512, 512
+FLOPS = 2 * S * K * H + 2 * N * S * H
+
+F32 = mybir.dt.float32
+BF16 = mybir.dt.bfloat16
+I32 = mybir.dt.int32
+U32 = mybir.dt.uint32
+U16 = mybir.dt.uint16
+U8 = mybir.dt.uint8
+FP8X4 = mybir.dt.float8_e4m3fn_x4
+COPY = mybir.ActivationFunctionType.Copy
+MULT = mybir.AluOpType.mult
+ADD = mybir.AluOpType.add
+SUBTRACT = mybir.AluOpType.subtract
+
+P = 128
+PACK = 4
+HALVES = 2
+HALF = H // HALVES
+LIST_COLS = HALF // 16
+
+
+def tile_picked_tokkindadif_none_p_kernel(
+    tc, x_words, x_scales, wa, tab, gt, w1, offs, n1, n2, n3, n4, out
+):
+    nc = tc.nc
+    tiles = range(PACK)
+    halves = range(HALVES)
+
+    def cols(h):
+        return slice(h * HALF, (h + 1) * HALF)
+
+    def picked(window, offsets, h):
+        return window[:].indirect(offsets[:, h * LIST_COLS : (h + 1) * LIST_COLS])
+
+    with ExitStack() as ctx:
+        keep = ctx.enter_context(tc.tile_pool(name="keep", bufs=1))
+        psum = ctx.enter_context(tc.psum_pool(name="psum", bufs=1))
+
+        def load_list(name, src):
+            lst = keep.tile([P, H // 16], U16, name=name)
+            nc.sync.dma_start(lst[:], src)
+            return lst
+
+        tab_rows = tab.rearrange("(p t) n -> p t n", t=PACK)
+        wa_rows = wa.rearrange("(p j) n -> p j n", j=PACK)
+        tab_sb = [keep.tile([P, H], F32, name=f"tab{t}") for t in tiles]
+        wa_sb = [keep.tile([P, PACK, HALF], F32, name=f"wa{h}") for h in halves]
+        w1_sb = keep.tile([P, PACK, N], F32, name="w1_sb")
+        gt_sb = keep.tile([P, PACK], F32, name="gt_sb")
+        x_word_table = keep.tile([P, T], U32, name="x_word_table")
+        x_scale_table = keep.tile([P, T], U8, name="x_scale_table")
+
+        nc.vector.memset(x_scale_table[:].bitcast(I32), 0)
+        n1_sb = load_list("n1_sb", n1)
+        nc.sync.dma_start(tab_sb[0][:], tab_rows[:, 0, :])
+        nc.sync.dma_start(gt_sb[:], gt.rearrange("(p t) o -> p (t o)", t=PACK))
+        nc.sync.dma_start(tab_sb[1][:], tab_rows[:, 1, :])
+        n2_sb = load_list("n2_sb", n2)
+        offs_sb = load_list("offs_sb", offs)
+        nc.sync.dma_start(
+            x_word_table[:].bitcast(I32), x_words[0].rearrange("p n r -> p (n r)").bitcast(I32)
+        )
+        nc.sync.dma_start(tab_sb[2][:], tab_rows[:, 2, :])
+        for q in range(4):
+            nc.sync.dma_start(
+                x_scale_table[32 * q : 32 * q + 4, :].bitcast(I32),
+                x_scales[0, 4 * q : 4 * q + 4, :].bitcast(I32),
+            )
+        nc.sync.dma_start(wa_sb[0][:], wa_rows[:, :, cols(0)])
+        nc.sync.dma_start(tab_sb[3][:], tab_rows[:, 3, :])
+        nc.sync.dma_start(wa_sb[1][:], wa_rows[:, :, cols(1)])
+        n3_sb = load_list("n3_sb", n3)
+        nc.sync.dma_start(w1_sb[:], w1.rearrange("(p j) n -> p j n", j=PACK))
+        n4_sb = load_list("n4_sb", n4)
+
+        gtab_sb = [keep.tile([P, H], F32, name=f"gtab{t}") for t in tiles]
+        factor = [keep.tile([P, PACK, HALF], F32, name=f"factor{h}") for h in halves]
+        addend = [keep.tile([P, PACK, HALF], F32, name=f"addend{h}") for h in halves]
+
+        def look_up_tab(t):
+            nc.vector.tensor_scalar(gtab_sb[t][:], tab_sb[t][:], gt_sb[:, t : t + 1], None, MULT)
+            for h in halves:
+                nc.scalar.activation(factor[h][:, t, :], picked(tab_sb[t], n1_sb, h), COPY)
+            for h in halves:
+                if t == 0:
+                    nc.vector.tensor_copy(addend[h][:, t, :], picked(gtab_sb[t], n2_sb, h))
+                else:
+                    nc.scalar.activation(addend[h][:, t, :], picked(gtab_sb[t], n2_sb, h), COPY)
+
+        look_up_tab(0)
+        look_up_tab(1)
+
+        x_codes = keep.tile([P, S], U32, name="x_codes", align_bytes=64)
+        x_bytes = keep.tile([P, S], U8, name="x_bytes", align_bytes=64)
+        nc.vector.tensor_copy(
+            x_codes[:].rearrange("p (t m) -> p m t", t=PACK), x_word_table[:].indirect(offs_sb[:])
+        )
+        nc.vector.tensor_copy(
+            x_bytes[:].rearrange("p (t m) -> p m t", t=PACK), x_scale_table[:].indirect(offs_sb[:])
+        )
+        look_up_tab(2)
+
+        wa_bf = [keep.tile([P, HALF * PACK], BF16, name=f"wa_bf{h}", align_bytes=64) for h in halves]
+        wa_codes = [keep.tile([P, HALF], U32, name=f"wa_codes{h}", align_bytes=64) for h in halves]
+        wa_bytes = [keep.tile([P, HALF], U8, name=f"wa_bytes{h}", align_bytes=64) for h in halves]
+        for h in halves:
+            nc.vector.tensor_copy(
+                wa_bf[h][:].rearrange("p (c i j) -> p c j i", i=4, j=PACK),
+                wa_sb[h][:].rearrange("p j (c i) -> p c j i", i=4),
+            )
+        for h in halves:
+            nc.vector.quantize_mx(wa_codes[h][:].bitcast(FP8X4), wa_bytes[h][:], wa_bf[h][:])
+        look_up_tab(3)
+
+        y_ps = [psum.tile([P, H], F32, name=f"y_ps{t}") for t in tiles]
+        for t in tiles:
+            for h in halves:
+                nc.tensor.matmul_mx(
+                    y_ps[t][:, cols(h)],
+                    lhsT=x_codes[:, t * P : (t + 1) * P].bitcast(FP8X4),
+                    lhsT_scale=x_bytes[:, t * P : (t + 1) * P],
+                    rhs=wa_codes[h][:].bitcast(FP8X4),
+                    rhs_scale=wa_bytes[h][:],
+                    start=True,
+                    stop=True,
+                )
+        gy_sb = [keep.tile([P, H], F32, name=f"gy{t}") for t in tiles]
+        for t in tiles:
+            nc.scalar.activation(gy_sb[t][:], y_ps[t][:], COPY, scale=gt_sb[:, t : t + 1])
+
+        w1_bf = keep.tile([P, N * PACK], BF16, name="w1_bf", align_bytes=64)
+        w1_codes = keep.tile([P, N], U32, name="w1_codes", align_bytes=64)
+        w1_bytes = keep.tile([P, N], U8, name="w1_bytes", align_bytes=64)
+        w1_dealt = w1_bf[:].rearrange("p (t m j) -> p m j t", t=PACK, j=PACK)
+        w1_read = w1_sb[:].rearrange("p j (m t) -> p m j t", t=PACK)
+
+        product = [keep.tile([P, PACK, HALF], F32, name=f"product{h}") for h in halves]
+        y_picked = keep.tile([P, PACK, HALF], F32, name="y_picked")
+        z_bf = [keep.tile([P, HALF * PACK], BF16, name=f"z_bf{h}", align_bytes=64) for h in halves]
+        z_codes = [keep.tile([P, HALF], U32, name=f"z_codes{h}", align_bytes=64) for h in halves]
+        z_bytes = [keep.tile([P, HALF], U8, name=f"z_bytes{h}", align_bytes=64) for h in halves]
+
+        def sum_z(h):
+            nc.vector.tensor_tensor(
+                z_bf[h][:].rearrange("p (c i t) -> p c t i", i=2, t=PACK),
+                product[h][:].rearrange("p t (c i) -> p c t i", i=2),
+                addend[h][:].rearrange("p t (c i) -> p c t i", i=2),
+                ADD,
+            )
+
+        def quantize_z(h):
+            nc.vector.quantize_mx(z_codes[h][:].bitcast(FP8X4), z_bytes[h][:], z_bf[h][:])
+
+        nc.vector.tensor_copy(w1_dealt[:, : P // 2], w1_read[:, : P // 2])
+        nc.vector.tensor_copy(w1_dealt[:, P // 2 :], w1_read[:, P // 2 :])
+        for t in tiles:
+            nc.vector.tensor_tensor(product[0][:, t, :], picked(gy_sb[t], n3_sb, 0), factor[0][:, t, :], MULT)
+        for t in tiles:
+            nc.scalar.activation(y_picked[:, t, :], picked(gy_sb[t], n3_sb, 1), COPY)
+        nc.vector.quantize_mx(w1_codes[:].bitcast(FP8X4), w1_bytes[:], w1_bf[:])
+        sum_z(0)
+        nc.vector.tensor_tensor(product[1][:, :2, :], y_picked[:, :2, :], factor[1][:, :2, :], MULT)
+        quantize_z(0)
+        nc.vector.tensor_tensor(product[1][:, 2:, :], y_picked[:, 2:, :], factor[1][:, 2:, :], MULT)
+        sum_z(1)
+        quantize_z(1)
+
+        h_ps = [psum.tile([P, H], F32, name=f"h_ps{t}") for t in tiles]
+        neg_h = [keep.tile([P, H], F32, name=f"neg_h{t}") for t in tiles]
+        other = [keep.tile([P, H], F32, name=f"other{t}") for t in tiles]
+        result = [keep.tile([P, H], F32, name=f"result{t}") for t in tiles]
+        out_rows = out.rearrange("(p t) n -> p t n", t=PACK)
+        fused = [(t, h) for t in tiles for h in halves][:5]
+        for h in halves:
+            for t in tiles:
+                nc.tensor.matmul_mx(
+                    h_ps[t][:, cols(h)],
+                    lhsT=w1_codes[:, t * P : (t + 1) * P].bitcast(FP8X4),
+                    lhsT_scale=w1_bytes[:, t * P : (t + 1) * P],
+                    rhs=z_codes[h][:].bitcast(FP8X4),
+                    rhs_scale=z_bytes[h][:],
+                    start=True,
+                    stop=True,
+                )
+            for t in tiles:
+                nc.scalar.activation(neg_h[t][:, cols(h)], h_ps[t][:, cols(h)], COPY, scale=-1.0)
+            for t in tiles:
+                if (t, h) in fused:
+                    nc.scalar.copy(other[t][:, cols(h)], h_ps[t][:, cols(h)])
+        for t in tiles:
+            for h in halves:
+                if (t, h) in fused:
+                    nc.vector.tensor_tensor(result[t][:, cols(h)], picked(neg_h[t], n4_sb, h), other[t][:, cols(h)], ADD)
+                else:
+                    nc.scalar.activation(other[t][:, cols(h)], picked(neg_h[t], n4_sb, h), COPY)
+                    nc.vector.tensor_tensor(result[t][:, cols(h)], other[t][:, cols(h)], neg_h[t][:, cols(h)], SUBTRACT)
+            if t < 2:
+                nc.sync.dma_start(out_rows[:, t, :], result[t][:])
+            else:
+                for h in halves:
+                    nc.sync.dma_start(out_rows[:, t, cols(h)], result[t][:, cols(h)])

@@ -19,9 +19,14 @@ SUBTRACT = mybir.AluOpType.subtract
 
 P = 128
 PACK = 4
-HALVES = 2
-HALF = H // HALVES
-LIST_COLS = HALF // 16
+QUADRANTS = 4
+PER_COLUMN = 16
+LINE = 4
+PAIR = 2
+HALF = H // 2
+QUARTER = H // 4
+LAST = PACK - 1
+ADDENDS_ON_VECTOR = ((0, 0), (0, 1), (1, 0))
 
 
 def tile_picked_tokkindadif_none_p_kernel(
@@ -29,28 +34,40 @@ def tile_picked_tokkindadif_none_p_kernel(
 ):
     nc = tc.nc
     tiles = range(PACK)
-    halves = range(HALVES)
+    halves = [slice(0, HALF), slice(HALF, H)]
 
-    def cols(h):
-        return slice(h * HALF, (h + 1) * HALF)
+    def picked(window, offsets, columns):
+        return window[:].indirect(offsets[:, columns.start // PER_COLUMN : columns.stop // PER_COLUMN])
 
-    def picked(window, offsets, h):
-        return window[:].indirect(offsets[:, h * LIST_COLS : (h + 1) * LIST_COLS])
+    def planes(ap):
+        return ap.rearrange("p (t c) -> p t c", t=PACK)
 
     with ExitStack() as ctx:
         keep = ctx.enter_context(tc.tile_pool(name="keep", bufs=1))
         psum = ctx.enter_context(tc.psum_pool(name="psum", bufs=1))
 
         def load_list(name, src):
-            lst = keep.tile([P, H // 16], U16, name=name)
-            nc.sync.dma_start(lst[:], src)
-            return lst
+            offsets = keep.tile([P, H // PER_COLUMN], U16, name=name)
+            nc.sync.dma_start(offsets[:], src)
+            return offsets
+
+        def product_mx(bank, left_codes, left_bytes, t, right_codes, right_bytes):
+            nc.tensor.matmul_mx(
+                bank,
+                lhsT=left_codes[:, t * P : (t + 1) * P].bitcast(FP8X4),
+                lhsT_scale=left_bytes[:, t * P : (t + 1) * P],
+                rhs=right_codes[:].bitcast(FP8X4),
+                rhs_scale=right_bytes[:],
+                start=True,
+                stop=True,
+            )
 
         tab_rows = tab.rearrange("(p t) n -> p t n", t=PACK)
-        wa_rows = wa.rearrange("(p j) n -> p j n", j=PACK)
         tab_sb = [keep.tile([P, H], F32, name=f"tab{t}") for t in tiles]
-        wa_sb = [keep.tile([P, PACK, HALF], F32, name=f"wa{h}") for h in halves]
-        w1_sb = keep.tile([P, PACK, N], F32, name="w1_sb")
+        wa_sb = keep.tile([P, PACK * H], F32, name="wa_sb")
+        shared = keep.tile([P, (PACK + LAST) * H], F32, name="shared")
+        addend = planes(shared[:, : PACK * H])
+        w1_sb = shared[:, LAST * H :]
         gt_sb = keep.tile([P, PACK], F32, name="gt_sb")
         x_word_table = keep.tile([P, T], U32, name="x_word_table")
         x_scale_table = keep.tile([P, T], U8, name="x_scale_table")
@@ -61,146 +78,151 @@ def tile_picked_tokkindadif_none_p_kernel(
         nc.sync.dma_start(gt_sb[:], gt.rearrange("(p t) o -> p (t o)", t=PACK))
         nc.sync.dma_start(tab_sb[1][:], tab_rows[:, 1, :])
         n2_sb = load_list("n2_sb", n2)
+        nc.sync.dma_start(wa_sb[:], wa.rearrange("(p j) n -> p (j n)", j=PACK))
         offs_sb = load_list("offs_sb", offs)
-        nc.sync.dma_start(
-            x_word_table[:].bitcast(I32), x_words[0].rearrange("p n r -> p (n r)").bitcast(I32)
-        )
-        nc.sync.dma_start(tab_sb[2][:], tab_rows[:, 2, :])
-        for q in range(4):
+        for q in range(QUADRANTS):
             nc.sync.dma_start(
                 x_scale_table[32 * q : 32 * q + 4, :].bitcast(I32),
                 x_scales[0, 4 * q : 4 * q + 4, :].bitcast(I32),
             )
-        nc.sync.dma_start(wa_sb[0][:], wa_rows[:, :, cols(0)])
-        nc.sync.dma_start(tab_sb[3][:], tab_rows[:, 3, :])
-        nc.sync.dma_start(wa_sb[1][:], wa_rows[:, :, cols(1)])
+        nc.sync.dma_start(tab_sb[2][:], tab_rows[:, 2, :])
+        nc.sync.dma_start(x_word_table[:].bitcast(I32), x_words[0].rearrange("p n r -> p (n r)").bitcast(I32))
+        nc.sync.dma_start(tab_sb[LAST][:], tab_rows[:, LAST, :])
         n3_sb = load_list("n3_sb", n3)
-        nc.sync.dma_start(w1_sb[:], w1.rearrange("(p j) n -> p j n", j=PACK))
+        nc.sync.dma_start(w1_sb, w1.rearrange("(p j) n -> p (j n)", j=PACK))
         n4_sb = load_list("n4_sb", n4)
 
-        gtab_sb = [keep.tile([P, H], F32, name=f"gtab{t}") for t in tiles]
-        factor = [keep.tile([P, PACK, HALF], F32, name=f"factor{h}") for h in halves]
-        addend = [keep.tile([P, PACK, HALF], F32, name=f"addend{h}") for h in halves]
+        weighted_tab = [keep.tile([P, H], F32, name=f"weighted_tab{t}") for t in tiles]
+        factor = [keep.tile([P, PACK, HALF], F32, name=f"factor{h}") for h in range(2)]
 
-        def look_up_tab(t):
-            nc.vector.tensor_scalar(gtab_sb[t][:], tab_sb[t][:], gt_sb[:, t : t + 1], None, MULT)
-            for h in halves:
-                nc.scalar.activation(factor[h][:, t, :], picked(tab_sb[t], n1_sb, h), COPY)
-            for h in halves:
-                if t == 0:
-                    nc.vector.tensor_copy(addend[h][:, t, :], picked(gtab_sb[t], n2_sb, h))
+        def weigh_tab_and_look_up_factor(t):
+            nc.vector.tensor_scalar(weighted_tab[t][:], tab_sb[t][:], gt_sb[:, t : t + 1], None, MULT)
+            for h, columns in enumerate(halves):
+                nc.scalar.activation(factor[h][:, t, :], picked(tab_sb[t], n1_sb, columns), COPY)
+
+        def look_up_addend(t):
+            for h, columns in enumerate(halves):
+                if (t, h) in ADDENDS_ON_VECTOR:
+                    nc.vector.tensor_copy(addend[:, t, columns], picked(weighted_tab[t], n2_sb, columns))
                 else:
-                    nc.scalar.activation(addend[h][:, t, :], picked(gtab_sb[t], n2_sb, h), COPY)
+                    nc.scalar.activation(addend[:, t, columns], picked(weighted_tab[t], n2_sb, columns), COPY)
 
-        look_up_tab(0)
-        look_up_tab(1)
+        for t in range(2):
+            weigh_tab_and_look_up_factor(t)
+            look_up_addend(t)
+
+        wa_bf = keep.tile([P, H * PACK], BF16, name="wa_bf", align_bytes=64)
+        wa_codes = keep.tile([P, H], U32, name="wa_codes", align_bytes=64)
+        wa_bytes = keep.tile([P, H], U8, name="wa_bytes", align_bytes=64)
+        nc.vector.tensor_copy(
+            wa_bf[:].rearrange("p (c i j) -> p c j i", i=LINE, j=PACK),
+            wa_sb[:].rearrange("p (j c i) -> p c j i", j=PACK, i=LINE),
+        )
+        nc.vector.quantize_mx(wa_codes[:].bitcast(FP8X4), wa_bytes[:], wa_bf[:])
+        weigh_tab_and_look_up_factor(2)
+        look_up_addend(2)
 
         x_codes = keep.tile([P, S], U32, name="x_codes", align_bytes=64)
         x_bytes = keep.tile([P, S], U8, name="x_bytes", align_bytes=64)
-        nc.vector.tensor_copy(
-            x_codes[:].rearrange("p (t m) -> p m t", t=PACK), x_word_table[:].indirect(offs_sb[:])
-        )
-        nc.vector.tensor_copy(
-            x_bytes[:].rearrange("p (t m) -> p m t", t=PACK), x_scale_table[:].indirect(offs_sb[:])
-        )
-        look_up_tab(2)
+        nc.vector.tensor_copy(x_bytes[:].rearrange("p (t m) -> p m t", t=PACK), x_scale_table[:].indirect(offs_sb[:]))
+        nc.vector.tensor_copy(x_codes[:].rearrange("p (t m) -> p m t", t=PACK), x_word_table[:].indirect(offs_sb[:]))
+        weigh_tab_and_look_up_factor(LAST)
 
-        wa_bf = [keep.tile([P, HALF * PACK], BF16, name=f"wa_bf{h}", align_bytes=64) for h in halves]
-        wa_codes = [keep.tile([P, HALF], U32, name=f"wa_codes{h}", align_bytes=64) for h in halves]
-        wa_bytes = [keep.tile([P, HALF], U8, name=f"wa_bytes{h}", align_bytes=64) for h in halves]
-        for h in halves:
-            nc.vector.tensor_copy(
-                wa_bf[h][:].rearrange("p (c i j) -> p c j i", i=4, j=PACK),
-                wa_sb[h][:].rearrange("p j (c i) -> p c j i", i=4),
-            )
-        for h in halves:
-            nc.vector.quantize_mx(wa_codes[h][:].bitcast(FP8X4), wa_bytes[h][:], wa_bf[h][:])
-        look_up_tab(3)
-
-        y_ps = [psum.tile([P, H], F32, name=f"y_ps{t}") for t in tiles]
+        y_banks = [psum.tile([P, H], F32, name=f"y_bank{t}") for t in tiles]
         for t in tiles:
-            for h in halves:
-                nc.tensor.matmul_mx(
-                    y_ps[t][:, cols(h)],
-                    lhsT=x_codes[:, t * P : (t + 1) * P].bitcast(FP8X4),
-                    lhsT_scale=x_bytes[:, t * P : (t + 1) * P],
-                    rhs=wa_codes[h][:].bitcast(FP8X4),
-                    rhs_scale=wa_bytes[h][:],
-                    start=True,
-                    stop=True,
-                )
-        gy_sb = [keep.tile([P, H], F32, name=f"gy{t}") for t in tiles]
+            product_mx(y_banks[t][:], x_codes, x_bytes, t, wa_codes, wa_bytes)
+        weighted_y = [keep.tile([P, H], F32, name=f"weighted_y{t}") for t in tiles]
         for t in tiles:
-            nc.scalar.activation(gy_sb[t][:], y_ps[t][:], COPY, scale=gt_sb[:, t : t + 1])
+            nc.scalar.activation(weighted_y[t][:], y_banks[t][:], COPY, scale=gt_sb[:, t : t + 1])
 
         w1_bf = keep.tile([P, N * PACK], BF16, name="w1_bf", align_bytes=64)
         w1_codes = keep.tile([P, N], U32, name="w1_codes", align_bytes=64)
         w1_bytes = keep.tile([P, N], U8, name="w1_bytes", align_bytes=64)
-        w1_dealt = w1_bf[:].rearrange("p (t m j) -> p m j t", t=PACK, j=PACK)
-        w1_read = w1_sb[:].rearrange("p j (m t) -> p m j t", t=PACK)
+        nc.vector.tensor_copy(
+            w1_bf[:].rearrange("p (t a i j) -> p a t j i", t=PACK, i=LINE, j=PACK),
+            w1_sb.rearrange("p (j a t i) -> p a t j i", j=PACK, t=PACK, i=LINE),
+        )
+        look_up_addend(LAST)
 
-        product = [keep.tile([P, PACK, HALF], F32, name=f"product{h}") for h in halves]
-        y_picked = keep.tile([P, PACK, HALF], F32, name="y_picked")
-        z_bf = [keep.tile([P, HALF * PACK], BF16, name=f"z_bf{h}", align_bytes=64) for h in halves]
-        z_codes = [keep.tile([P, HALF], U32, name=f"z_codes{h}", align_bytes=64) for h in halves]
-        z_bytes = [keep.tile([P, HALF], U8, name=f"z_bytes{h}", align_bytes=64) for h in halves]
+        pieces = [halves[0], slice(HALF, HALF + QUARTER), slice(HALF + QUARTER, H)]
+        z_bf = keep.tile([P, H * PACK], BF16, name="z_bf", align_bytes=64)
+        z_codes = [keep.tile([P, c.stop - c.start], U32, name=f"z_codes{c.start}", align_bytes=64) for c in pieces]
+        z_bytes = [keep.tile([P, c.stop - c.start], U8, name=f"z_bytes{c.start}", align_bytes=64) for c in pieces]
 
-        def sum_z(h):
+        def z_piece(n):
+            return z_bf[:, pieces[n].start * PACK : pieces[n].stop * PACK]
+
+        def sum_z(n, product):
             nc.vector.tensor_tensor(
-                z_bf[h][:].rearrange("p (c i t) -> p c t i", i=2, t=PACK),
-                product[h][:].rearrange("p t (c i) -> p c t i", i=2),
-                addend[h][:].rearrange("p t (c i) -> p c t i", i=2),
+                z_piece(n).rearrange("p (c i t) -> p c t i", i=PAIR, t=PACK),
+                product.rearrange("p t (c i) -> p c t i", i=PAIR),
+                addend[:, :, pieces[n]].rearrange("p t (c i) -> p c t i", i=PAIR),
                 ADD,
             )
 
-        def quantize_z(h):
-            nc.vector.quantize_mx(z_codes[h][:].bitcast(FP8X4), z_bytes[h][:], z_bf[h][:])
+        def quantize_z(n):
+            nc.vector.quantize_mx(z_codes[n][:].bitcast(FP8X4), z_bytes[n][:], z_piece(n))
 
-        nc.vector.tensor_copy(w1_dealt[:, : P // 2], w1_read[:, : P // 2])
-        nc.vector.tensor_copy(w1_dealt[:, P // 2 :], w1_read[:, P // 2 :])
+        half_product = planes(w1_sb[:, 2 * H :])
         for t in tiles:
-            nc.vector.tensor_tensor(product[0][:, t, :], picked(gy_sb[t], n3_sb, 0), factor[0][:, t, :], MULT)
-        for t in tiles:
-            nc.scalar.activation(y_picked[:, t, :], picked(gy_sb[t], n3_sb, 1), COPY)
+            nc.vector.tensor_tensor(
+                half_product[:, t, :], picked(weighted_y[t], n3_sb, halves[0]), factor[0][:, t, :], MULT
+            )
         nc.vector.quantize_mx(w1_codes[:].bitcast(FP8X4), w1_bytes[:], w1_bf[:])
-        sum_z(0)
-        nc.vector.tensor_tensor(product[1][:, :2, :], y_picked[:, :2, :], factor[1][:, :2, :], MULT)
-        quantize_z(0)
-        nc.vector.tensor_tensor(product[1][:, 2:, :], y_picked[:, 2:, :], factor[1][:, 2:, :], MULT)
-        sum_z(1)
-        quantize_z(1)
 
-        h_ps = [psum.tile([P, H], F32, name=f"h_ps{t}") for t in tiles]
+        y_picked = [planes(w1_sb[:, H : 2 * H]), planes(weighted_tab[LAST][:])]
+        quarter_product = [factor[0][:, 2:, :].rearrange("p u (v c) -> p (u v) c", c=QUARTER), y_picked[0]]
+        for q in range(2):
+            for t in tiles:
+                nc.scalar.activation(y_picked[q][:, t, :], picked(weighted_y[t], n3_sb, pieces[1 + q]), COPY)
+
+        def multiply_quarter(q):
+            nc.vector.tensor_tensor(
+                quarter_product[q], y_picked[q], factor[1][:, :, q * QUARTER : (q + 1) * QUARTER], MULT
+            )
+
+        sum_z(0, half_product)
+        multiply_quarter(0)
+        quantize_z(0)
+        sum_z(1, quarter_product[0])
+        multiply_quarter(1)
+        quantize_z(1)
+        sum_z(2, quarter_product[1])
+        quantize_z(2)
+
+        h_banks = [psum.tile([P, H], F32, name=f"h_bank{t}") for t in tiles]
+        banks_of_piece = [h_banks, y_banks, h_banks]
         neg_h = [keep.tile([P, H], F32, name=f"neg_h{t}") for t in tiles]
-        other = [keep.tile([P, H], F32, name=f"other{t}") for t in tiles]
         result = [keep.tile([P, H], F32, name=f"result{t}") for t in tiles]
-        out_rows = out.rearrange("(p t) n -> p t n", t=PACK)
-        fused = [(t, h) for t in tiles for h in halves][:5]
-        for h in halves:
+        neg_h_picked = keep.tile([P, PACK, HALF], F32, name="neg_h_picked")
+        out_rows = out.rearrange("(a t i) n -> t a i n", t=PACK, i=LINE)
+        for n, columns in enumerate(pieces):
             for t in tiles:
-                nc.tensor.matmul_mx(
-                    h_ps[t][:, cols(h)],
-                    lhsT=w1_codes[:, t * P : (t + 1) * P].bitcast(FP8X4),
-                    lhsT_scale=w1_bytes[:, t * P : (t + 1) * P],
-                    rhs=z_codes[h][:].bitcast(FP8X4),
-                    rhs_scale=z_bytes[h][:],
-                    start=True,
-                    stop=True,
-                )
+                product_mx(banks_of_piece[n][t][:, columns], w1_codes, w1_bytes, t, z_codes[n], z_bytes[n])
             for t in tiles:
-                nc.scalar.activation(neg_h[t][:, cols(h)], h_ps[t][:, cols(h)], COPY, scale=-1.0)
-            for t in tiles:
-                if (t, h) in fused:
-                    nc.scalar.copy(other[t][:, cols(h)], h_ps[t][:, cols(h)])
+                nc.scalar.activation(neg_h[t][:, columns], banks_of_piece[n][t][:, columns], COPY, scale=-1.0)
+
+        neg_h_copy = addend[:, :, halves[1]]
+
+        def store(t, columns):
+            nc.sync.dma_start(out_rows[t][:, :, columns], result[t][:, columns])
+
+        def first_half(t):
+            nc.vector.tensor_tensor(
+                result[t][:, halves[0]], picked(neg_h[t], n4_sb, halves[0]), neg_h_copy[:, t, :], SUBTRACT
+            )
+            store(t, halves[0])
+
+        def second_half(t):
+            nc.vector.tensor_tensor(result[t][:, halves[1]], neg_h_picked[:, t, :], neg_h[t][:, halves[1]], SUBTRACT)
+            store(t, halves[1])
+
         for t in tiles:
-            for h in halves:
-                if (t, h) in fused:
-                    nc.vector.tensor_tensor(result[t][:, cols(h)], picked(neg_h[t], n4_sb, h), other[t][:, cols(h)], ADD)
-                else:
-                    nc.scalar.activation(other[t][:, cols(h)], picked(neg_h[t], n4_sb, h), COPY)
-                    nc.vector.tensor_tensor(result[t][:, cols(h)], other[t][:, cols(h)], neg_h[t][:, cols(h)], SUBTRACT)
-            if t < 2:
-                nc.sync.dma_start(out_rows[:, t, :], result[t][:])
-            else:
-                for h in halves:
-                    nc.sync.dma_start(out_rows[:, t, cols(h)], result[t][:, cols(h)])
+            nc.vector.tensor_copy(neg_h_copy[:, t, :], neg_h[t][:, halves[0]])
+        for t in tiles:
+            nc.scalar.activation(neg_h_picked[:, t, :], picked(neg_h[t], n4_sb, halves[1]), COPY)
+        first_half(0)
+        for t in tiles:
+            if t < LAST:
+                first_half(t + 1)
+            second_half(t)

from contextlib import ExitStack

import concourse.mybir as mybir

K, T, S, N, H = 512, 2048, 512, 512, 512
FLOPS = 2 * S * K * H + 2 * N * S * H

F32 = mybir.dt.float32
BF16 = mybir.dt.bfloat16
I32 = mybir.dt.int32
U32 = mybir.dt.uint32
U16 = mybir.dt.uint16
U8 = mybir.dt.uint8
FP8X4 = mybir.dt.float8_e4m3fn_x4
COPY = mybir.ActivationFunctionType.Copy
MULT = mybir.AluOpType.mult
ADD = mybir.AluOpType.add
SUBTRACT = mybir.AluOpType.subtract

P = 128
PACK = 4
QUADRANTS = 4
PER_COLUMN = 16
LINE = 4
PAIR = 2
HALF = H // 2
QUARTER = H // 4
LAST = PACK - 1
ADDENDS_ON_VECTOR = ((0, 0), (0, 1), (1, 0))


def tile_picked_tokkindadif_none_p_kernel(
    tc, x_words, x_scales, wa, tab, gt, w1, offs, n1, n2, n3, n4, out
):
    nc = tc.nc
    tiles = range(PACK)
    halves = [slice(0, HALF), slice(HALF, H)]

    def picked(window, offsets, columns):
        return window[:].indirect(offsets[:, columns.start // PER_COLUMN : columns.stop // PER_COLUMN])

    def planes(ap):
        return ap.rearrange("p (t c) -> p t c", t=PACK)

    with ExitStack() as ctx:
        keep = ctx.enter_context(tc.tile_pool(name="keep", bufs=1))
        psum = ctx.enter_context(tc.psum_pool(name="psum", bufs=1))

        def load_list(name, src):
            offsets = keep.tile([P, H // PER_COLUMN], U16, name=name)
            nc.sync.dma_start(offsets[:], src)
            return offsets

        def product_mx(bank, left_codes, left_bytes, t, right_codes, right_bytes):
            nc.tensor.matmul_mx(
                bank,
                lhsT=left_codes[:, t * P : (t + 1) * P].bitcast(FP8X4),
                lhsT_scale=left_bytes[:, t * P : (t + 1) * P],
                rhs=right_codes[:].bitcast(FP8X4),
                rhs_scale=right_bytes[:],
                start=True,
                stop=True,
            )

        tab_rows = tab.rearrange("(p t) n -> p t n", t=PACK)
        tab_sb = [keep.tile([P, H], F32, name=f"tab{t}") for t in tiles]
        wa_sb = keep.tile([P, PACK * H], F32, name="wa_sb")
        shared = keep.tile([P, (PACK + LAST) * H], F32, name="shared")
        addend = planes(shared[:, : PACK * H])
        w1_sb = shared[:, LAST * H :]
        gt_sb = keep.tile([P, PACK], F32, name="gt_sb")
        x_word_table = keep.tile([P, T], U32, name="x_word_table")
        x_scale_table = keep.tile([P, T], U8, name="x_scale_table")

        nc.vector.memset(x_scale_table[:].bitcast(I32), 0)
        n1_sb = load_list("n1_sb", n1)
        nc.sync.dma_start(tab_sb[0][:], tab_rows[:, 0, :])
        nc.sync.dma_start(gt_sb[:], gt.rearrange("(p t) o -> p (t o)", t=PACK))
        nc.sync.dma_start(tab_sb[1][:], tab_rows[:, 1, :])
        n2_sb = load_list("n2_sb", n2)
        nc.sync.dma_start(wa_sb[:], wa.rearrange("(p j) n -> p (j n)", j=PACK))
        offs_sb = load_list("offs_sb", offs)
        for q in range(QUADRANTS):
            nc.sync.dma_start(
                x_scale_table[32 * q : 32 * q + 4, :].bitcast(I32),
                x_scales[0, 4 * q : 4 * q + 4, :].bitcast(I32),
            )
        nc.sync.dma_start(tab_sb[2][:], tab_rows[:, 2, :])
        nc.sync.dma_start(x_word_table[:].bitcast(I32), x_words[0].rearrange("p n r -> p (n r)").bitcast(I32))
        nc.sync.dma_start(tab_sb[LAST][:], tab_rows[:, LAST, :])
        n3_sb = load_list("n3_sb", n3)
        nc.sync.dma_start(w1_sb, w1.rearrange("(p j) n -> p (j n)", j=PACK))
        n4_sb = load_list("n4_sb", n4)

        weighted_tab = [keep.tile([P, H], F32, name=f"weighted_tab{t}") for t in tiles]
        factor = [keep.tile([P, PACK, HALF], F32, name=f"factor{h}") for h in range(2)]

        def weigh_tab_and_look_up_factor(t):
            nc.vector.tensor_scalar(weighted_tab[t][:], tab_sb[t][:], gt_sb[:, t : t + 1], None, MULT)
            for h, columns in enumerate(halves):
                nc.scalar.activation(factor[h][:, t, :], picked(tab_sb[t], n1_sb, columns), COPY)

        def look_up_addend(t):
            for h, columns in enumerate(halves):
                if (t, h) in ADDENDS_ON_VECTOR:
                    nc.vector.tensor_copy(addend[:, t, columns], picked(weighted_tab[t], n2_sb, columns))
                else:
                    nc.scalar.activation(addend[:, t, columns], picked(weighted_tab[t], n2_sb, columns), COPY)

        for t in range(2):
            weigh_tab_and_look_up_factor(t)
            look_up_addend(t)

        wa_bf = keep.tile([P, H * PACK], BF16, name="wa_bf", align_bytes=64)
        wa_codes = keep.tile([P, H], U32, name="wa_codes", align_bytes=64)
        wa_bytes = keep.tile([P, H], U8, name="wa_bytes", align_bytes=64)
        nc.vector.tensor_copy(
            wa_bf[:].rearrange("p (c i j) -> p c j i", i=LINE, j=PACK),
            wa_sb[:].rearrange("p (j c i) -> p c j i", j=PACK, i=LINE),
        )
        nc.vector.quantize_mx(wa_codes[:].bitcast(FP8X4), wa_bytes[:], wa_bf[:])
        weigh_tab_and_look_up_factor(2)
        look_up_addend(2)

        x_codes = keep.tile([P, S], U32, name="x_codes", align_bytes=64)
        x_bytes = keep.tile([P, S], U8, name="x_bytes", align_bytes=64)
        nc.vector.tensor_copy(x_bytes[:].rearrange("p (t m) -> p m t", t=PACK), x_scale_table[:].indirect(offs_sb[:]))
        nc.vector.tensor_copy(x_codes[:].rearrange("p (t m) -> p m t", t=PACK), x_word_table[:].indirect(offs_sb[:]))
        weigh_tab_and_look_up_factor(LAST)

        y_banks = [psum.tile([P, H], F32, name=f"y_bank{t}") for t in tiles]
        for t in tiles:
            product_mx(y_banks[t][:], x_codes, x_bytes, t, wa_codes, wa_bytes)
        weighted_y = [keep.tile([P, H], F32, name=f"weighted_y{t}") for t in tiles]
        for t in tiles:
            nc.scalar.activation(weighted_y[t][:], y_banks[t][:], COPY, scale=gt_sb[:, t : t + 1])

        w1_bf = keep.tile([P, N * PACK], BF16, name="w1_bf", align_bytes=64)
        w1_codes = keep.tile([P, N], U32, name="w1_codes", align_bytes=64)
        w1_bytes = keep.tile([P, N], U8, name="w1_bytes", align_bytes=64)
        nc.vector.tensor_copy(
            w1_bf[:].rearrange("p (t a i j) -> p a t j i", t=PACK, i=LINE, j=PACK),
            w1_sb.rearrange("p (j a t i) -> p a t j i", j=PACK, t=PACK, i=LINE),
        )
        look_up_addend(LAST)

        pieces = [halves[0], slice(HALF, HALF + QUARTER), slice(HALF + QUARTER, H)]
        z_bf = keep.tile([P, H * PACK], BF16, name="z_bf", align_bytes=64)
        z_codes = [keep.tile([P, c.stop - c.start], U32, name=f"z_codes{c.start}", align_bytes=64) for c in pieces]
        z_bytes = [keep.tile([P, c.stop - c.start], U8, name=f"z_bytes{c.start}", align_bytes=64) for c in pieces]

        def z_piece(n):
            return z_bf[:, pieces[n].start * PACK : pieces[n].stop * PACK]

        def sum_z(n, product):
            nc.vector.tensor_tensor(
                z_piece(n).rearrange("p (c i t) -> p c t i", i=PAIR, t=PACK),
                product.rearrange("p t (c i) -> p c t i", i=PAIR),
                addend[:, :, pieces[n]].rearrange("p t (c i) -> p c t i", i=PAIR),
                ADD,
            )

        def quantize_z(n):
            nc.vector.quantize_mx(z_codes[n][:].bitcast(FP8X4), z_bytes[n][:], z_piece(n))

        half_product = planes(w1_sb[:, 2 * H :])
        for t in tiles:
            nc.vector.tensor_tensor(
                half_product[:, t, :], picked(weighted_y[t], n3_sb, halves[0]), factor[0][:, t, :], MULT
            )
        nc.vector.quantize_mx(w1_codes[:].bitcast(FP8X4), w1_bytes[:], w1_bf[:])

        y_picked = [planes(w1_sb[:, H : 2 * H]), planes(weighted_tab[LAST][:])]
        quarter_product = [factor[0][:, 2:, :].rearrange("p u (v c) -> p (u v) c", c=QUARTER), y_picked[0]]
        for q in range(2):
            for t in tiles:
                nc.scalar.activation(y_picked[q][:, t, :], picked(weighted_y[t], n3_sb, pieces[1 + q]), COPY)

        def multiply_quarter(q):
            nc.vector.tensor_tensor(
                quarter_product[q], y_picked[q], factor[1][:, :, q * QUARTER : (q + 1) * QUARTER], MULT
            )

        sum_z(0, half_product)
        multiply_quarter(0)
        quantize_z(0)
        sum_z(1, quarter_product[0])
        multiply_quarter(1)
        quantize_z(1)
        sum_z(2, quarter_product[1])
        quantize_z(2)

        h_banks = [psum.tile([P, H], F32, name=f"h_bank{t}") for t in tiles]
        banks_of_piece = [h_banks, y_banks, h_banks]
        neg_h = [keep.tile([P, H], F32, name=f"neg_h{t}") for t in tiles]
        result = [keep.tile([P, H], F32, name=f"result{t}") for t in tiles]
        neg_h_picked = keep.tile([P, PACK, HALF], F32, name="neg_h_picked")
        out_rows = out.rearrange("(a t i) n -> t a i n", t=PACK, i=LINE)
        for n, columns in enumerate(pieces):
            for t in tiles:
                product_mx(banks_of_piece[n][t][:, columns], w1_codes, w1_bytes, t, z_codes[n], z_bytes[n])
            for t in tiles:
                nc.scalar.activation(neg_h[t][:, columns], banks_of_piece[n][t][:, columns], COPY, scale=-1.0)

        neg_h_copy = addend[:, :, halves[1]]

        def store(t, columns):
            nc.sync.dma_start(out_rows[t][:, :, columns], result[t][:, columns])

        def first_half(t):
            nc.vector.tensor_tensor(
                result[t][:, halves[0]], picked(neg_h[t], n4_sb, halves[0]), neg_h_copy[:, t, :], SUBTRACT
            )
            store(t, halves[0])

        def second_half(t):
            nc.vector.tensor_tensor(result[t][:, halves[1]], neg_h_picked[:, t, :], neg_h[t][:, halves[1]], SUBTRACT)
            store(t, halves[1])

        for t in tiles:
            nc.vector.tensor_copy(neg_h_copy[:, t, :], neg_h[t][:, halves[0]])
        for t in tiles:
            nc.scalar.activation(neg_h_picked[:, t, :], picked(neg_h[t], n4_sb, halves[1]), COPY)
        first_half(0)
        for t in tiles:
            if t < LAST:
                first_half(t + 1)
            second_half(t)
